import numpy as np, ml_dtypes
CORES = [3,11,19,27,131,139,147,155]
N = 8
T = 16
ROUTE = [[[5,1,6],[7,5,4],[6,0,1],[0,4,7],[0,5,6],[3,5,7],[3,0,5],[5,3,0],[2,5,1],[5,6,4],[1,3,5],[3,7,1],[6,5,4],[3,4,5],[0,7,4],[6,4,3]],[[1,3,6],[7,4,2],[7,0,2],[1,4,7],[6,5,0],[4,7,5],[0,3,5],[6,2,7],[3,2,1],[2,5,6],[1,4,7],[0,1,6],[1,5,0],[4,0,2],[2,7,3],[7,0,1]],[[2,5,0],[3,0,6],[1,0,4],[0,4,3],[2,4,1],[7,5,0],[1,6,5],[4,7,2],[1,7,0],[6,1,4],[7,1,3],[5,2,7],[0,1,7],[7,4,0],[3,4,0],[4,7,6]],[[1,7,5],[4,6,3],[1,4,6],[5,1,6],[5,0,6],[4,3,7],[4,7,5],[0,2,7],[0,6,7],[7,4,1],[4,1,2],[6,5,7],[6,3,4],[5,0,6],[7,2,6],[0,2,1]],[[7,6,0],[3,7,2],[6,0,2],[1,6,0],[6,7,5],[1,6,2],[7,1,6],[5,6,3],[5,6,1],[2,7,5],[1,4,7],[1,5,0],[6,1,3],[3,4,1],[0,4,2],[7,3,6]],[[7,0,6],[3,5,1],[5,1,2],[1,3,2],[1,2,6],[5,1,6],[4,3,5],[1,5,0],[3,2,5],[1,5,6],[5,6,7],[6,7,0],[3,5,0],[6,1,7],[1,5,6],[0,5,2]],[[6,7,1],[3,0,7],[5,2,4],[1,0,4],[0,4,5],[3,5,2],[3,7,0],[4,6,1],[6,5,7],[4,0,7],[3,4,6],[0,6,3],[6,5,1],[5,7,1],[1,7,4],[1,2,3]],[[3,6,7],[3,4,0],[1,0,4],[3,5,7],[3,5,6],[0,6,5],[5,0,1],[0,4,3],[0,6,7],[3,1,4],[6,5,0],[1,4,0],[7,6,5],[1,4,6],[5,1,6],[6,2,4]]]
YW = 57
def setup_inputs(rng):
    return {"x": rng.standard_normal((N, 128, T), dtype=np.float32).astype(ml_dtypes.bfloat16)}
def reference(x):
    y = np.full((N, 128, YW), np.nan, x.dtype)
    fill = [0] * N
    for r in range(N):
        for t in range(T):
            for e in ROUTE[r][t]:
                y[e][:, fill[e]] = x[r][:, t]
                fill[e] += 1
    return {"y": y}

@@ -1,0 +1,44 @@
+SCRATCH = {
+    "xs": ("sbuf", [128, 16], "bfloat16"),
+    "land": ("sbuf", [128, 57], "bfloat16"),
+}
+SEMAPHORES = ["loaded", "arrived", "own", "stored"]
+
+
+def token_runs(route, n):
+    fill = [0] * n
+    runs = [[[] for _ in range(n)] for _ in range(n)]
+    for r in range(n):
+        for t, experts in enumerate(route[r]):
+            for e in experts:
+                lst = runs[r][e]
+                if lst and lst[-1][0] + lst[-1][1] == t:
+                    lst[-1] = (lst[-1][0], lst[-1][1] + 1, lst[-1][2])
+                else:
+                    lst.append((t, 1, fill[e]))
+                fill[e] += 1
+    return runs, fill
+
+
+def rank_program(g, core, T, topo):
+    rank = T.rank_of(core)
+    if rank is None:
+        return
+    n = len(T.cores)
+    runs, count = token_runs(T.tables["ROUTE"], n)
+    g.dma_start(T.xs[:], T.x[:]).then_inc(T.sem.loaded, 16)
+    g.wait_ge(T.sem.loaded, 16)
+    total = 0
+    for k in range(1, n):
+        e = (rank + k) % n
+        rid, pid = topo.addr(T.cores[e], core)
+        for t0, w, col in runs[rank][e]:
+            g.remote_dma(T.land[:, col:col + w], T.xs[:, t0:t0 + w], T.sem.arrived, T.sem.arrived, pid, rid, 0xFF)
+            total += 8
+    for t0, w, col in runs[rank][rank]:
+        g.dma_start(T.land[:, col:col + w], T.xs[:, t0:t0 + w]).then_inc(T.sem.own, 16)
+    total += sum(8 * len(runs[r][rank]) for r in range(n) if r != rank)
+    g.wait_ge(T.sem.own, 16 * len(runs[rank][rank]))
+    g.wait_ge(T.sem.arrived, total)
+    g.dma_start(T.y[:, 0:count[rank]], T.land[:, 0:count[rank]]).then_inc(T.sem.stored, 16)
+    g.wait_ge(T.sem.stored, 16)

@@ -1,8 +1,16 @@
+import concourse.bass as bass
+
 SCRATCH = {
     "xs": ("sbuf", [128, 16], "bfloat16"),
     "land": ("sbuf", [128, 57], "bfloat16"),
 }
-SEMAPHORES = ["loaded", "arrived", "own", "stored"]
+SEMAPHORES = ["loaded", "got", "arrived", "stored"]
+
+MODE = "side"
+RANK_CORE = 3
+PORT_CORES = (3, 2, 6, 7)
+PLANE_CORES = (0, 1, 4)
+SELF_CORE = 5
 
 
 def token_runs(route, n):
@@ -20,25 +28,100 @@ def token_runs(route, n):
     return runs, fill
 
 
+def shares(k, engines):
+    p = 1
+    while 2 * p * k <= engines:
+        p *= 2
+    more = (engines - p * k) // p
+    return [2 * p] * more + [p] * (k - more)
+
+
+def calls_for(rs, engines, mode):
+    rs = sorted(rs, key=lambda q: -q[1])
+    calls = []
+    if mode == "side":
+        bit, by_w = 0, {}
+        for q, s in zip(rs, shares(len(rs), engines)):
+            by_w.setdefault(q[1], []).append(q + (((1 << s) - 1) << bit,))
+            bit += s
+        calls = [by_w[w] for w in sorted(by_w)]
+    elif mode == "stack":
+        by_w = {}
+        for q in rs:
+            by_w.setdefault(q[1], []).append(q)
+        for w in sorted(by_w):
+            bit, c = 0, []
+            for q, s in zip(by_w[w], shares(len(by_w[w]), engines)):
+                c.append(q + (((1 << s) - 1) << bit,))
+                bit += s
+            calls.append(c)
+    elif mode == "each":
+        calls = [[q + ((1 << engines) - 1,)] for q in rs]
+    elif mode == "singles":
+        cols = [(t0 + i, 1, col + i) for t0, w, col in rs for i in range(w)]
+        ncall = -(-len(cols) // engines)
+        per = -(-len(cols) // ncall)
+        for a in range(0, len(cols), per):
+            part, bit, c = cols[a:a + per], 0, []
+            for q, s in zip(part, shares(len(part), engines)):
+                c.append(q + (((1 << s) - 1) << bit,))
+                bit += s
+            calls.append(c)
+    return calls
+
+
+def roles(r, cores, runs, topo):
+    n = len(cores)
+    other = [e for e in range(n) if topo.chip(cores[e]) % 2 != topo.chip(cores[r]) % 2]
+    same = [e for e in range(n) if e != r and e not in other]
+    other.sort(key=lambda e: -len(runs[r][e]))
+    role = dict(zip(PORT_CORES, other))
+    role.update(zip(PLANE_CORES, same))
+    role[SELF_CORE] = r
+    return role
+
+
+def popcount(m):
+    return bin(m).count("1")
+
+
 def rank_program(g, core, T, topo):
-    rank = T.rank_of(core)
-    if rank is None:
+    base = core - core % 8
+    r = T.rank_of(base + RANK_CORE)
+    if r is None:
         return
     n = len(T.cores)
     runs, count = token_runs(T.tables["ROUTE"], n)
+    e = roles(r, T.cores, runs, topo)[core % 8]
+    mine = calls_for(runs[r][e], 16 if e == r else 8, MODE)
+    sent = sum(popcount(q[3]) for c in mine for q in c)
+    rid, pid = topo.addr(T.cores[e], core)
+
+    def scatter(local_sem):
+        for c in mine:
+            g.remote_dma_fused([bass.RemoteDMATransfer(dst_ids=[bass.DstId(rid=rid, pnc=pid)], dma_engine_mask=m,
+                                                       remote_sem=T.sem.arrived, src=T.xs[:, t0:t0 + w],
+                                                       dst=T.land[:, col:col + w]) for t0, w, col, m in c],
+                               local_sem=local_sem)
+
+    if core % 8 != RANK_CORE:
+        g.wait_ge(T.sem.got, 16)
+        scatter(T.sem.got)
+        g.wait_ge(T.sem.got, 16 + sent)
+        return
+
     g.dma_start(T.xs[:], T.x[:]).then_inc(T.sem.loaded, 16)
     g.wait_ge(T.sem.loaded, 16)
-    total = 0
-    for k in range(1, n):
-        e = (rank + k) % n
-        rid, pid = topo.addr(T.cores[e], core)
-        for t0, w, col in runs[rank][e]:
-            g.remote_dma(T.land[:, col:col + w], T.xs[:, t0:t0 + w], T.sem.arrived, T.sem.arrived, pid, rid, 0xFF)
-            total += 8
-    for t0, w, col in runs[rank][rank]:
-        g.dma_start(T.land[:, col:col + w], T.xs[:, t0:t0 + w]).then_inc(T.sem.own, 16)
-    total += sum(8 * len(runs[r][rank]) for r in range(n) if r != rank)
-    g.wait_ge(T.sem.own, 16 * len(runs[rank][rank]))
+    helpers = [base + k for k in range(8) if k != RANK_CORE]
+    ids = [topo.addr(h, core) for h in helpers]
+    g.remote_dma_fused([bass.RemoteDMATransfer(dst_ids=[bass.DstId(rid=a, pnc=b) for a, b in ids],
+                                               dma_engine_mask=0xFFFF, remote_sem=T.sem.got,
+                                               srcs=[T.xs[:]], dsts=[T.xs[:] for _ in ids])],
+                       local_sem=T.sem.arrived)
+    scatter(T.sem.arrived)
+    total = 16 + sent
+    for s in range(n):
+        total += sum(popcount(q[3]) for c in calls_for(runs[s][r], 16 if s == r else 8, MODE) for q in c)
     g.wait_ge(T.sem.arrived, total)
-    g.dma_start(T.y[:, 0:count[rank]], T.land[:, 0:count[rank]]).then_inc(T.sem.stored, 16)
+    g.dma_start(T.y[:, 0:count[r]], T.land[:, 0:count[r]]).then_inc(T.sem.stored, 16)
     g.wait_ge(T.sem.stored, 16)

@@ -6,11 +6,12 @@ SCRATCH = {
 }
 SEMAPHORES = ["loaded", "got", "arrived", "stored"]
 
-MODE = "side"
 RANK_CORE = 3
-PORT_CORES = (3, 2, 6, 7)
-PLANE_CORES = (0, 1, 4)
-SELF_CORE = 5
+PORT_HELPERS = (2, 6, 7)
+PLANE_HELPERS = (0, 1, 4, 5)
+RANK_CALLS = 3
+HEAD_START = 16
+CACHE = {}
 
 
 def token_runs(route, n):
@@ -29,6 +30,8 @@ def token_runs(route, n):
 
 
 def shares(k, engines):
+    if k == 0:
+        return []
     p = 1
     while 2 * p * k <= engines:
         p *= 2
@@ -36,49 +39,113 @@ def shares(k, engines):
     return [2 * p] * more + [p] * (k - more)
 
 
-def calls_for(rs, engines, mode):
-    rs = sorted(rs, key=lambda q: -q[1])
-    calls = []
-    if mode == "side":
-        bit, by_w = 0, {}
-        for q, s in zip(rs, shares(len(rs), engines)):
-            by_w.setdefault(q[1], []).append(q + (((1 << s) - 1) << bit,))
-            bit += s
-        calls = [by_w[w] for w in sorted(by_w)]
-    elif mode == "stack":
-        by_w = {}
-        for q in rs:
-            by_w.setdefault(q[1], []).append(q)
-        for w in sorted(by_w):
-            bit, c = 0, []
-            for q, s in zip(by_w[w], shares(len(by_w[w]), engines)):
-                c.append(q + (((1 << s) - 1) << bit,))
-                bit += s
-            calls.append(c)
-    elif mode == "each":
-        calls = [[q + ((1 << engines) - 1,)] for q in rs]
-    elif mode == "singles":
-        cols = [(t0 + i, 1, col + i) for t0, w, col in rs for i in range(w)]
-        ncall = -(-len(cols) // engines)
-        per = -(-len(cols) // ncall)
-        for a in range(0, len(cols), per):
-            part, bit, c = cols[a:a + per], 0, []
-            for q, s in zip(part, shares(len(part), engines)):
-                c.append(q + (((1 << s) - 1) << bit,))
-                bit += s
-            calls.append(c)
-    return calls
+def rows(k):
+    return 128 // min(shares(k, 8)) if k else 0
 
 
-def roles(r, cores, runs, topo):
+def multisets(lo, hi, k):
+    if k == 0:
+        return [()]
+    return [(a,) + m for a in range(lo, hi + 1) for m in multisets(a, hi, k - 1)]
+
+
+def cuts(w, allowed):
+    if w == 0:
+        return [()]
+    out = []
+    for i, a in enumerate(allowed):
+        if a <= w:
+            out += [(a,) + c for c in cuts(w - a, allowed[i:])]
+    return out
+
+
+def spread(k, slots):
+    return [k // slots + (1 if i < k % slots else 0) for i in range(slots)]
+
+
+def split_by_width(widths, helpers, rank_calls):
+    best = None
+    wide = sorted(set(w for w in widths if w > 1))
+    for extra in [()] + [(a,) for a in range(2, max(widths) + 1)] + [(a, b) for a in wide for b in wide if a < b]:
+        allowed = (1,) + extra
+        reach = {tuple(0 for _ in allowed): ()}
+        for w in widths:
+            nxt = {}
+            for c in cuts(w, allowed):
+                for cnt, how in reach.items():
+                    key = tuple(v + c.count(a) for v, a in zip(cnt, allowed))
+                    if key not in nxt:
+                        nxt[key] = how + (c,)
+            reach = nxt
+        for hs in multisets(0, len(allowed) - 1, helpers):
+            for rs in multisets(0, len(allowed) - 1, rank_calls):
+                for cnt, how in reach.items():
+                    hplan, rplan, ok = [], [], True
+                    for i, (a, c) in enumerate(zip(allowed, cnt)):
+                        nh, nr = hs.count(i), rs.count(i)
+                        to_h = min(c, 4 * nh)
+                        if c - to_h > 8 * nr:
+                            ok = False
+                            break
+                        hplan += [(a, k) for k in spread(to_h, nh)] if nh else []
+                        rplan += [(a, k) for k in spread(c - to_h, nr)] if nr else []
+                    if not ok:
+                        continue
+                    score = (max(max(rows(k) for _, k in hplan) + HEAD_START, sum(rows(k) for _, k in rplan)),
+                             sum(1 for _, k in rplan if k), sum(cnt))
+                    if best is None or score < best[0]:
+                        best = (score, how, hplan, rplan)
+    return best[1], best[2], best[3]
+
+
+def deal(group, helpers, rank_calls):
+    how, hplan, rplan = split_by_width([q[2] for q in group], helpers, rank_calls)
+    pool = {}
+    for (e, t0, w, col), cut in zip(group, how):
+        at = 0
+        for a in cut:
+            pool.setdefault(a, []).append((e, t0 + at, a, col + at))
+            at += a
+    return [[[pool[a].pop() for _ in range(k)] for a, k in plan] for plan in (hplan, rplan)]
+
+
+def masked(blocks, first_engine):
+    out, bit = [], first_engine
+    for q, s in zip(blocks, shares(len(blocks), 8)):
+        out.append(q + (((1 << s) - 1) << bit,))
+        bit += s
+    return out
+
+
+def plan_rank(r, cores, runs, topo):
     n = len(cores)
-    other = [e for e in range(n) if topo.chip(cores[e]) % 2 != topo.chip(cores[r]) % 2]
-    same = [e for e in range(n) if e != r and e not in other]
-    other.sort(key=lambda e: -len(runs[r][e]))
-    role = dict(zip(PORT_CORES, other))
-    role.update(zip(PLANE_CORES, same))
-    role[SELF_CORE] = r
-    return role
+    par = [topo.chip(c) % 2 for c in cores]
+    other = [(e,) + q for e in range(n) if par[e] != par[r] for q in runs[r][e]]
+    same = [(e,) + q for e in range(n) if par[e] == par[r] and e != r for q in runs[r][e]]
+    port, mine = deal(other, len(PORT_HELPERS), RANK_CALLS)
+    plane, _ = deal(same, len(PLANE_HELPERS), 0)
+    off = dict(zip(PORT_HELPERS + PLANE_HELPERS, port + plane))
+    off = {k: b for k, b in off.items() if b}
+    have = sorted(set(b[0][2] for b in off.values()), reverse=True)
+    own = {k: [] for k in off}
+    for t0, w, col in runs[r][r]:
+        at = 0
+        while at < w:
+            a = [v for v in have if v <= w - at][0]
+            k = min((k for k in off if off[k][0][2] == a), key=lambda k: (len(own[k]), k))
+            own[k].append((r, t0 + at, a, col + at))
+            at += a
+    plan = {k: [masked(off[k], 0) + masked(own[k], 8)] for k in off}
+    plan[RANK_CORE] = [masked(b, 0) for b in mine if b]
+    return plan
+
+
+def plans(T, topo):
+    if "p" not in CACHE:
+        n = len(T.cores)
+        runs, count = token_runs(T.tables["ROUTE"], n)
+        CACHE["p"] = ([plan_rank(r, T.cores, runs, topo) for r in range(n)], count)
+    return CACHE["p"]
 
 
 def popcount(m):
@@ -90,19 +157,21 @@ def rank_program(g, core, T, topo):
     r = T.rank_of(base + RANK_CORE)
     if r is None:
         return
-    n = len(T.cores)
-    runs, count = token_runs(T.tables["ROUTE"], n)
-    e = roles(r, T.cores, runs, topo)[core % 8]
-    mine = calls_for(runs[r][e], 16 if e == r else 8, MODE)
-    sent = sum(popcount(q[3]) for c in mine for q in c)
-    rid, pid = topo.addr(T.cores[e], core)
+    plan, count = plans(T, topo)
+    mine = plan[r].get(core % 8, [])
+    if not mine and core % 8 != RANK_CORE:
+        return
+    sent = sum(popcount(q[4]) for c in mine for q in c)
 
     def scatter(local_sem):
         for c in mine:
-            g.remote_dma_fused([bass.RemoteDMATransfer(dst_ids=[bass.DstId(rid=rid, pnc=pid)], dma_engine_mask=m,
-                                                       remote_sem=T.sem.arrived, src=T.xs[:, t0:t0 + w],
-                                                       dst=T.land[:, col:col + w]) for t0, w, col, m in c],
-                               local_sem=local_sem)
+            trs = []
+            for e, t0, w, col, m in c:
+                rid, pid = topo.addr(T.cores[e], core)
+                trs.append(bass.RemoteDMATransfer(dst_ids=[bass.DstId(rid=rid, pnc=pid)], dma_engine_mask=m,
+                                                  remote_sem=T.sem.arrived, src=T.xs[:, t0:t0 + w],
+                                                  dst=T.land[:, col:col + w]))
+            g.remote_dma_fused(trs, local_sem=local_sem)
 
     if core % 8 != RANK_CORE:
         g.wait_ge(T.sem.got, 16)
@@ -112,16 +181,13 @@ def rank_program(g, core, T, topo):
 
     g.dma_start(T.xs[:], T.x[:]).then_inc(T.sem.loaded, 16)
     g.wait_ge(T.sem.loaded, 16)
-    helpers = [base + k for k in range(8) if k != RANK_CORE]
-    ids = [topo.addr(h, core) for h in helpers]
+    ids = [topo.addr(base + k, core) for k in sorted(plan[r]) if k != RANK_CORE]
     g.remote_dma_fused([bass.RemoteDMATransfer(dst_ids=[bass.DstId(rid=a, pnc=b) for a, b in ids],
                                                dma_engine_mask=0xFFFF, remote_sem=T.sem.got,
                                                srcs=[T.xs[:]], dsts=[T.xs[:] for _ in ids])],
                        local_sem=T.sem.arrived)
     scatter(T.sem.arrived)
-    total = 16 + sent
-    for s in range(n):
-        total += sum(popcount(q[3]) for c in calls_for(runs[s][r], 16 if s == r else 8, MODE) for q in c)
+    total = 16 + sent + sum(popcount(q[4]) for p in plan for cs in p.values() for c in cs for q in c if q[0] == r)
     g.wait_ge(T.sem.arrived, total)
     g.dma_start(T.y[:, 0:count[r]], T.land[:, 0:count[r]]).then_inc(T.sem.stored, 16)
     g.wait_ge(T.sem.stored, 16)

@@ -4,7 +4,7 @@ SCRATCH = {
     "xs": ("sbuf", [128, 16], "bfloat16"),
     "land": ("sbuf", [128, 57], "bfloat16"),
 }
-SEMAPHORES = ["loaded", "got", "arrived", "stored"]
+SEMAPHORES = ["loaded", "own", "got", "arrived", "stored"]
 
 RANK_CORE = 3
 PORT_HELPERS = (2, 6, 7)
@@ -109,8 +109,8 @@ def deal(group, helpers, rank_calls):
     return [[[pool[a].pop() for _ in range(k)] for a, k in plan] for plan in (hplan, rplan)]
 
 
-def masked(blocks, first_engine):
-    out, bit = [], first_engine
+def masked(blocks):
+    out, bit = [], 0
     for q, s in zip(blocks, shares(len(blocks), 8)):
         out.append(q + (((1 << s) - 1) << bit,))
         bit += s
@@ -124,19 +124,8 @@ def plan_rank(r, cores, runs, topo):
     same = [(e,) + q for e in range(n) if par[e] == par[r] and e != r for q in runs[r][e]]
     port, mine = deal(other, len(PORT_HELPERS), RANK_CALLS)
     plane, _ = deal(same, len(PLANE_HELPERS), 0)
-    off = dict(zip(PORT_HELPERS + PLANE_HELPERS, port + plane))
-    off = {k: b for k, b in off.items() if b}
-    have = sorted(set(b[0][2] for b in off.values()), reverse=True)
-    own = {k: [] for k in off}
-    for t0, w, col in runs[r][r]:
-        at = 0
-        while at < w:
-            a = [v for v in have if v <= w - at][0]
-            k = min((k for k in off if off[k][0][2] == a), key=lambda k: (len(own[k]), k))
-            own[k].append((r, t0 + at, a, col + at))
-            at += a
-    plan = {k: [masked(off[k], 0) + masked(own[k], 8)] for k in off}
-    plan[RANK_CORE] = [masked(b, 0) for b in mine if b]
+    plan = {k: [masked(b)] for k, b in zip(PORT_HELPERS + PLANE_HELPERS, port + plane) if b}
+    plan[RANK_CORE] = [masked(b) for b in mine if b]
     return plan
 
 
@@ -144,7 +133,7 @@ def plans(T, topo):
     if "p" not in CACHE:
         n = len(T.cores)
         runs, count = token_runs(T.tables["ROUTE"], n)
-        CACHE["p"] = ([plan_rank(r, T.cores, runs, topo) for r in range(n)], count)
+        CACHE["p"] = ([plan_rank(r, T.cores, runs, topo) for r in range(n)], runs, count)
     return CACHE["p"]
 
 
@@ -157,7 +146,7 @@ def rank_program(g, core, T, topo):
     r = T.rank_of(base + RANK_CORE)
     if r is None:
         return
-    plan, count = plans(T, topo)
+    plan, runs, count = plans(T, topo)
     mine = plan[r].get(core % 8, [])
     if not mine and core % 8 != RANK_CORE:
         return
@@ -180,6 +169,9 @@ def rank_program(g, core, T, topo):
         return
 
     g.dma_start(T.xs[:], T.x[:]).then_inc(T.sem.loaded, 16)
+    for t0, w, col in runs[r][r]:
+        g.dma_start(T.land[:, col:col + w], T.x[:, t0:t0 + w],
+                    allow_slow_non_contiguous=(w == 1)).then_inc(T.sem.own, 16)
     g.wait_ge(T.sem.loaded, 16)
     ids = [topo.addr(base + k, core) for k in sorted(plan[r]) if k != RANK_CORE]
     g.remote_dma_fused([bass.RemoteDMATransfer(dst_ids=[bass.DstId(rid=a, pnc=b) for a, b in ids],
@@ -188,6 +180,7 @@ def rank_program(g, core, T, topo):
                        local_sem=T.sem.arrived)
     scatter(T.sem.arrived)
     total = 16 + sent + sum(popcount(q[4]) for p in plan for cs in p.values() for c in cs for q in c if q[0] == r)
+    g.wait_ge(T.sem.own, 16 * len(runs[r][r]))
     g.wait_ge(T.sem.arrived, total)
     g.dma_start(T.y[:, 0:count[r]], T.land[:, 0:count[r]]).then_inc(T.sem.stored, 16)
     g.wait_ge(T.sem.stored, 16)

import concourse.bass as bass

SCRATCH = {
    "xs": ("sbuf", [128, 16], "bfloat16"),
    "land": ("sbuf", [128, 57], "bfloat16"),
}
SEMAPHORES = ["loaded", "own", "got", "arrived", "stored"]

RANK_CORE = 3
PORT_HELPERS = (2, 6, 7)
PLANE_HELPERS = (0, 1, 4, 5)
RANK_CALLS = 3
HEAD_START = 16
CACHE = {}


def token_runs(route, n):
    fill = [0] * n
    runs = [[[] for _ in range(n)] for _ in range(n)]
    for r in range(n):
        for t, experts in enumerate(route[r]):
            for e in experts:
                lst = runs[r][e]
                if lst and lst[-1][0] + lst[-1][1] == t:
                    lst[-1] = (lst[-1][0], lst[-1][1] + 1, lst[-1][2])
                else:
                    lst.append((t, 1, fill[e]))
                fill[e] += 1
    return runs, fill


def shares(k, engines):
    if k == 0:
        return []
    p = 1
    while 2 * p * k <= engines:
        p *= 2
    more = (engines - p * k) // p
    return [2 * p] * more + [p] * (k - more)


def rows(k):
    return 128 // min(shares(k, 8)) if k else 0


def multisets(lo, hi, k):
    if k == 0:
        return [()]
    return [(a,) + m for a in range(lo, hi + 1) for m in multisets(a, hi, k - 1)]


def cuts(w, allowed):
    if w == 0:
        return [()]
    out = []
    for i, a in enumerate(allowed):
        if a <= w:
            out += [(a,) + c for c in cuts(w - a, allowed[i:])]
    return out


def spread(k, slots):
    return [k // slots + (1 if i < k % slots else 0) for i in range(slots)]


def split_by_width(widths, helpers, rank_calls):
    best = None
    wide = sorted(set(w for w in widths if w > 1))
    for extra in [()] + [(a,) for a in range(2, max(widths) + 1)] + [(a, b) for a in wide for b in wide if a < b]:
        allowed = (1,) + extra
        reach = {tuple(0 for _ in allowed): ()}
        for w in widths:
            nxt = {}
            for c in cuts(w, allowed):
                for cnt, how in reach.items():
                    key = tuple(v + c.count(a) for v, a in zip(cnt, allowed))
                    if key not in nxt:
                        nxt[key] = how + (c,)
            reach = nxt
        for hs in multisets(0, len(allowed) - 1, helpers):
            for rs in multisets(0, len(allowed) - 1, rank_calls):
                for cnt, how in reach.items():
                    hplan, rplan, ok = [], [], True
                    for i, (a, c) in enumerate(zip(allowed, cnt)):
                        nh, nr = hs.count(i), rs.count(i)
                        to_h = min(c, 4 * nh)
                        if c - to_h > 8 * nr:
                            ok = False
                            break
                        hplan += [(a, k) for k in spread(to_h, nh)] if nh else []
                        rplan += [(a, k) for k in spread(c - to_h, nr)] if nr else []
                    if not ok:
                        continue
                    score = (max(max(rows(k) for _, k in hplan) + HEAD_START, sum(rows(k) for _, k in rplan)),
                             sum(1 for _, k in rplan if k), sum(cnt))
                    if best is None or score < best[0]:
                        best = (score, how, hplan, rplan)
    return best[1], best[2], best[3]


def deal(group, helpers, rank_calls):
    how, hplan, rplan = split_by_width([q[2] for q in group], helpers, rank_calls)
    pool = {}
    for (e, t0, w, col), cut in zip(group, how):
        at = 0
        for a in cut:
            pool.setdefault(a, []).append((e, t0 + at, a, col + at))
            at += a
    return [[[pool[a].pop() for _ in range(k)] for a, k in plan] for plan in (hplan, rplan)]


def masked(blocks):
    out, bit = [], 0
    for q, s in zip(blocks, shares(len(blocks), 8)):
        out.append(q + (((1 << s) - 1) << bit,))
        bit += s
    return out


def plan_rank(r, cores, runs, topo):
    n = len(cores)
    par = [topo.chip(c) % 2 for c in cores]
    other = [(e,) + q for e in range(n) if par[e] != par[r] for q in runs[r][e]]
    same = [(e,) + q for e in range(n) if par[e] == par[r] and e != r for q in runs[r][e]]
    port, mine = deal(other, len(PORT_HELPERS), RANK_CALLS)
    plane, _ = deal(same, len(PLANE_HELPERS), 0)
    plan = {k: [masked(b)] for k, b in zip(PORT_HELPERS + PLANE_HELPERS, port + plane) if b}
    plan[RANK_CORE] = [masked(b) for b in mine if b]
    return plan


def plans(T, topo):
    if "p" not in CACHE:
        n = len(T.cores)
        runs, count = token_runs(T.tables["ROUTE"], n)
        CACHE["p"] = ([plan_rank(r, T.cores, runs, topo) for r in range(n)], runs, count)
    return CACHE["p"]


def popcount(m):
    return bin(m).count("1")


def rank_program(g, core, T, topo):
    base = core - core % 8
    r = T.rank_of(base + RANK_CORE)
    if r is None:
        return
    plan, runs, count = plans(T, topo)
    mine = plan[r].get(core % 8, [])
    if not mine and core % 8 != RANK_CORE:
        return
    sent = sum(popcount(q[4]) for c in mine for q in c)

    def scatter(local_sem):
        for c in mine:
            trs = []
            for e, t0, w, col, m in c:
                rid, pid = topo.addr(T.cores[e], core)
                trs.append(bass.RemoteDMATransfer(dst_ids=[bass.DstId(rid=rid, pnc=pid)], dma_engine_mask=m,
                                                  remote_sem=T.sem.arrived, src=T.xs[:, t0:t0 + w],
                                                  dst=T.land[:, col:col + w]))
            g.remote_dma_fused(trs, local_sem=local_sem)

    if core % 8 != RANK_CORE:
        g.wait_ge(T.sem.got, 16)
        scatter(T.sem.got)
        g.wait_ge(T.sem.got, 16 + sent)
        return

    g.dma_start(T.xs[:], T.x[:]).then_inc(T.sem.loaded, 16)
    for t0, w, col in runs[r][r]:
        g.dma_start(T.land[:, col:col + w], T.x[:, t0:t0 + w],
                    allow_slow_non_contiguous=(w == 1)).then_inc(T.sem.own, 16)
    g.wait_ge(T.sem.loaded, 16)
    ids = [topo.addr(base + k, core) for k in sorted(plan[r]) if k != RANK_CORE]
    g.remote_dma_fused([bass.RemoteDMATransfer(dst_ids=[bass.DstId(rid=a, pnc=b) for a, b in ids],
                                               dma_engine_mask=0xFFFF, remote_sem=T.sem.got,
                                               srcs=[T.xs[:]], dsts=[T.xs[:] for _ in ids])],
                       local_sem=T.sem.arrived)
    scatter(T.sem.arrived)
    total = 16 + sent + sum(popcount(q[4]) for p in plan for cs in p.values() for c in cs for q in c if q[0] == r)
    g.wait_ge(T.sem.own, 16 * len(runs[r][r]))
    g.wait_ge(T.sem.arrived, total)
    g.dma_start(T.y[:, 0:count[r]], T.land[:, 0:count[r]]).then_inc(T.sem.stored, 16)
    g.wait_ge(T.sem.stored, 16)
